import numpy as np
import ml_dtypes


def mxq(x, axis, fmt="e4m3"):
    dtype, down = {"e4m3": (ml_dtypes.float8_e4m3fn, 7), "e5m2": (ml_dtypes.float8_e5m2, 14)}[fmt]
    v = np.moveaxis(np.asarray(x, np.float32).astype(ml_dtypes.bfloat16).astype(np.float64), axis, -1)
    blocks = v.reshape(v.shape[:-1] + (-1, 32))
    amax = np.abs(blocks).max(-1, keepdims=True)
    byte = np.maximum(np.where(amax > 0, np.frexp(amax)[1] - 1 + 127, 0) - down, 1)
    scale = np.exp2(byte - 127.0)
    codes = (blocks / scale).astype(np.float32).astype(dtype).astype(np.float64)
    return np.moveaxis((codes * scale).reshape(v.shape), -1, axis)


WIDE = False


def mx_kscale(k):
    if not WIDE:
        return np.ones(k)
    levels = np.array([10, -10, 5, -5, 0])
    if k % 512:
        return np.exp2(np.random.permutation(np.resize(levels, k // 32))).repeat(32)
    a = np.empty((k // 512, 16))
    for p in range(k // 512):
        a[p, :8] = np.random.permutation(np.resize(levels, 8))
        for g in range(8):
            far = levels[np.abs(levels - a[p, g]) >= 10]
            a[p, g + 8] = far[np.random.randint(len(far))]
    return np.exp2(a.ravel()).repeat(32)


def f64(x):
    return np.asarray(x).astype(np.float64)


def striped(idx):
    return np.tile(idx.reshape(-1, 16).T, (8, 1)).astype(np.uint16)


def unstriped(offs):
    return offs[:16].T.reshape(-1).astype(np.int64)


E2M1 = np.array([0.0, 0.5, 1.0, 1.5, 2.0, 3.0, 4.0, 6.0, -0.0, -0.5, -1.0, -1.5, -2.0, -3.0, -4.0, -6.0])


def pack_weight(w, fmt):
    k, n = w.shape
    w = f64(np.asarray(w, np.float32).astype(ml_dtypes.bfloat16)).reshape(k // 32, 32, n)
    amax = np.abs(w).max(1)
    if fmt == "e4m3":
        byte = np.frexp(amax)[1] - 1 + 127 - 7
    else:
        mant, ex = np.frexp(amax / 6.0)
        byte = np.where(mant > 0.5, ex, ex - 1) + 127
    byte = np.clip(np.where(amax > 0, byte, 1), 1, 254)
    scaled = (w * np.exp2(127.0 - byte)[:, None, :]).reshape(k, n).astype(np.float32)
    by_word = np.ascontiguousarray(scaled.reshape(k // 512, 128, 4, n).transpose(0, 1, 3, 2))
    if fmt == "e4m3":
        words = by_word.astype(ml_dtypes.float8_e4m3fn).view(np.uint8)
    else:
        c = by_word.astype(ml_dtypes.float4_e2m1fn).view(np.uint8) & 0xF
        words = (c[..., 0::2] | (c[..., 1::2] << 4)).reshape(k // 512, 128, 2 * n)
    return np.ascontiguousarray(words), np.ascontiguousarray(byte.astype(np.uint8).reshape(k // 512, 16, n))


def unpack_weight(words, scales, fmt):
    g, _, n = scales.shape
    words = np.ascontiguousarray(words).reshape(g, 128, n, -1)
    if fmt == "e4m3":
        vals = words.view(ml_dtypes.float8_e4m3fn).astype(np.float64)
    else:
        nib = np.empty((g, 128, n, 4), np.uint8)
        nib[..., 0::2] = words & 0xF
        nib[..., 1::2] = words >> 4
        vals = E2M1[nib]
    vals = vals * np.repeat(np.exp2(scales.astype(np.float64) - 127.0), 8, axis=1)[..., None]
    return vals.transpose(0, 1, 3, 2).reshape(g * 512, n)


def gelu(v):
    return 0.5 * v * (1.0 + np.tanh(np.sqrt(2.0 / np.pi) * (v + 0.044715 * v**3)))


K, T, S, H, P, N = 1024, 4096, 1024, 1024, 512, 768

def setup_inputs():
    n = np.random.standard_normal
    s = mx_kscale(K)[:, None]
    u = mx_kscale(H)[:, None]
    tab_words, tab_scales = pack_weight(n((K, T)) * s, "e4m3")
    w4_words, w4_scales = pack_weight(n((H, N)) / np.sqrt(H) / u, "e2m1")
    return {
        "tab_words": tab_words, "tab_scales": tab_scales,
        "offs": striped(np.random.permutation(T)[:S]),
        "pos1": striped(np.random.permutation(S)[:P]),
        "pos2": striped(np.random.permutation(S)[:P]),
        "w1": (n((K, H)) / np.sqrt(K) / s).astype(np.float32),
        "gain": (np.exp(0.3 * n(H)) * u[:, 0]).astype(np.float32),
        "rim": (0.7 * n(H) * u[:, 0]).astype(np.float32),
        "reading": np.exp(0.4 * n((H, P))).astype(np.float32),
        "floor_level": (0.8 * n(H) * u[:, 0]).astype(np.float32),
        "wa": (n((H, N)) / np.sqrt(H) / u).astype(np.float32),
        "w4_words": w4_words, "w4_scales": w4_scales,
    }

def reference(tab_words, tab_scales, offs, pos1, pos2, w1, gain, rim, reading, floor_level, wa, w4_words, w4_scales):
    v = unpack_weight(tab_words, tab_scales, "e4m3")[:, unstriped(offs)]
    w4 = unpack_weight(w4_words, w4_scales, "e2m1")
    h = f64(gain)[:, None] * (mxq(f64(w1), 0, "e4m3").T @ v)
    xa = (h[:, unstriped(pos1)] + f64(rim)[:, None]) * f64(reading)
    xb = np.maximum(h[:, unstriped(pos2)], f64(floor_level)[:, None])
    ya = mxq(f64(wa), 0, "e4m3").T @ mxq(xa, 0, "e4m3")
    yb = w4.T @ mxq(xb, 0, "e4m3")
    both = ya * yb
    return both + ya

@@ -1,0 +1,303 @@
+from contextlib import ExitStack
+
+import concourse.mybir as mybir
+
+K, T, S, H, M, N = 1024, 4096, 1024, 1024, 512, 768
+FLOPS = 2 * K * H * S + 2 * 2 * H * N * M
+
+F32 = mybir.dt.float32
+BF16 = mybir.dt.bfloat16
+I32 = mybir.dt.int32
+U32 = mybir.dt.uint32
+U16 = mybir.dt.uint16
+U8 = mybir.dt.uint8
+FP8X4 = mybir.dt.float8_e4m3fn_x4
+FP4X4 = mybir.dt.float4_e2m1fn_x4
+ALU = mybir.AluOpType
+COPY = mybir.ActivationFunctionType.Copy
+
+P = 128
+PACK = 4
+PASS = P * PACK
+BANK = 512
+PASSES = 2
+N_TILES = N // P
+WA_COLS = N // 2
+M_HALF = M // 2
+VECTOR_SHARE = 80
+
+
+def tile_list_zone_edge_lawn_kernel(
+    tc, tab_words, tab_scales, offs, pos1, pos2, w1, gain, rim, reading, floor_level, wa, w4_words, w4_scales, out
+):
+    nc = tc.nc
+    with ExitStack() as ctx:
+        held = ctx.enter_context(tc.tile_pool(name="held", bufs=1))
+        ring = ctx.enter_context(tc.tile_pool(name="ring", bufs=2))
+        psum = ctx.enter_context(tc.psum_pool(name="psum", bufs=1))
+
+        def bank(i, shape):
+            return psum.tile(shape, F32, name="bank%d" % i, tag="bank%d" % i)
+
+        def slot_tile(slot, shape, dtype):
+            return held.tile(shape, dtype, name="slot_%s" % slot, tag="slot_%s" % slot, align_bytes=64)
+
+        offs_t = held.tile([P, S // 16], U16, name="offs_t")
+        pos1_t = held.tile([P, M // 16], U16, name="pos1_t")
+        pos2_t = held.tile([P, M // 16], U16, name="pos2_t")
+        tab_w = [held.tile([P, T], I32, name="tab_w%d" % a) for a in range(PASSES)]
+        tab_s = slot_tile("table", [P, T], U8)
+        v_s = held.tile([P, S], U8, name="v_s", align_bytes=64)
+        gain_t = held.tile([P, PASSES, PACK], F32, name="gain_t")
+        rim_t = held.tile([P, PASSES, PACK], F32, name="rim_t")
+        floor_t = held.tile([P, PASSES, PACK], F32, name="floor_t")
+        read_t = [held.tile([P, PACK, M], F32, name="read_t%d" % b) for b in range(PASSES)]
+        w4_w = held.tile([P, PASSES, 2 * N], U8, name="w4_w", align_bytes=64)
+        w4_s = held.tile([P, PASSES, N], U8, name="w4_s", align_bytes=64)
+        wa_w = [held.tile([P, N], U32, name="wa_w%d" % b, align_bytes=64) for b in range(PASSES)]
+        wa_s = [held.tile([P, N], U8, name="wa_s%d" % b, align_bytes=64) for b in range(PASSES)]
+        w1_s = [[held.tile([P, PASS], U8, name="w1_s%d%d" % (b, a), align_bytes=64) for a in range(PASSES)]
+                for b in range(PASSES)]
+        h = [[held.tile([P, S], F32, name="h%d%d" % (b, t)) for t in range(PACK)] for b in range(PASSES)]
+        xb_w = [held.tile([P, M], U32, name="xb_w%d" % b, align_bytes=64) for b in range(PASSES)]
+        xb_s = [held.tile([P, M], U8, name="xb_s%d" % b, align_bytes=64) for b in range(PASSES)]
+        xa_w = [held.tile([P, M], U32, name="xa_w%d" % b, align_bytes=64) for b in range(PASSES)]
+        xa_s = [held.tile([P, M], U8, name="xa_s%d" % b, align_bytes=64) for b in range(PASSES)]
+        res = held.tile([P, N_TILES, M], F32, name="res")
+
+        w1_w = [
+            [held.tile([P, PASS], U32, name="w1_w00", align_bytes=64), slot_tile("c", [P, PASS], U32)],
+            [slot_tile("a", [P, PASS], U32), slot_tile("b", [P, PASS], U32)],
+        ]
+
+        def raw_tile(cols):
+            return ring.tile([P, PACK, cols], F32, name="raw", tag="raw", bufs=4)
+
+        def pass_rows(x, g):
+            return x[g * PASS : (g + 1) * PASS, :].rearrange("(p j) c -> p j c", j=PACK)
+
+        nc.vector.memset(tab_s[:].bitcast(I32), 0)
+        nc.vector.memset(w4_s[:].rearrange("p a n -> p (a n)").bitcast(I32), 0)
+        for q in range(4):
+            nc.gpsimd.dma_start(
+                out=tab_s[32 * q : 32 * q + 8, :].bitcast(I32), in_=tab_scales[:, 4 * q : 4 * q + 4, :].bitcast(I32)
+            )
+        w1_raw = {}
+
+        def load_w1(b):
+            for a in range(PASSES):
+                w1_raw[b, a] = raw_tile(PASS)
+                nc.sync.dma_start(out=w1_raw[b, a][:], in_=pass_rows(w1, a)[:, :, b * PASS : (b + 1) * PASS])
+
+        nc.sync.dma_start(offs_t[:], offs)
+        nc.sync.dma_start(out=tab_w[0][:], in_=tab_words[0].rearrange("p t i -> p (t i)").bitcast(I32))
+        nc.sync.dma_start(pos2_t[:], pos2)
+        nc.sync.dma_start(pos1_t[:], pos1)
+        for vec_t, vec in ((gain_t, gain), (floor_t, floor_level), (rim_t, rim)):
+            nc.sync.dma_start(out=vec_t[:], in_=vec.rearrange("(b p t) -> p b t", b=PASSES, t=PACK))
+        nc.sync.dma_start(out=tab_w[1][:], in_=tab_words[1].rearrange("p t i -> p (t i)").bitcast(I32))
+        load_w1(0)
+        nc.sync.dma_start(out=read_t[0][:], in_=pass_rows(reading, 0))
+        load_w1(1)
+
+        nc.vector.tensor_copy(v_s[:], tab_s[:].indirect(offs_t[:]))
+        v_w = [held.tile([P, S], U32, name="v_w0", align_bytes=64), slot_tile("table", [P, S], U32)]
+        for a in range(PASSES):
+            nc.vector.tensor_copy(v_w[a][:], tab_w[a][:].bitcast(U32).indirect(offs_t[:]))
+
+        def round_w1(b, a, vector_share):
+            rounded = slot_tile({(0, 0): "d", (0, 1): "e", (1, 0): "c", (1, 1): "d"}[b, a], [P, PACK, P, PACK], BF16)
+            dst = rounded[:].rearrange("p t m j -> p m j t")
+            src = w1_raw[b, a][:].rearrange("p j (m t) -> p m j t", t=PACK)
+            if vector_share:
+                nc.vector.tensor_copy(out=dst[:, :vector_share], in_=src[:, :vector_share])
+            nc.scalar.activation(out=dst[:, vector_share:], in_=src[:, vector_share:], func=COPY)
+            return rounded[:].rearrange("p t m j -> p (t m j)")
+
+        def quantize(words, scales, values):
+            nc.vector.quantize_mx(out=words.bitcast(FP8X4), scales=scales, in_=values)
+
+        def quantize_w1(b, a, rounded, edges):
+            for lo, hi in zip(edges, edges[1:]):
+                quantize(w1_w[b][a][:, lo:hi], w1_s[b][a][:, lo:hi], rounded[:, PACK * lo : PACK * hi])
+
+        acc = {}
+
+        def first_stage_pass(b, t, a):
+            rows = slice(t * P, (t + 1) * P)
+            for half in range(2):
+                if a == 0:
+                    acc[b, t, half] = bank(2 * t + half, [P, BANK])
+                cols = slice(half * BANK, (half + 1) * BANK)
+                nc.tensor.matmul_mx(
+                    out=acc[b, t, half][:],
+                    lhsT=w1_w[b][a][:, rows].bitcast(FP8X4),
+                    lhsT_scale=w1_s[b][a][:, rows],
+                    rhs=v_w[a][:, cols].bitcast(FP8X4),
+                    rhs_scale=v_s[4 * a : P, cols],
+                    start=(a == 0),
+                    stop=(a == PASSES - 1),
+                )
+
+        def apply_gain(b, t, vector_helps):
+            g = gain_t[:, b, t : t + 1]
+            nc.scalar.activation(out=h[b][t][:, :BANK], in_=acc[b, t, 0][:], func=COPY, scale=g)
+            if vector_helps:
+                nc.vector.tensor_scalar_mul(h[b][t][:, BANK:], acc[b, t, 1][:], g)
+            else:
+                nc.scalar.activation(out=h[b][t][:, BANK:], in_=acc[b, t, 1][:], func=COPY, scale=g)
+
+        quantize_w1(0, 0, round_w1(0, 0, VECTOR_SHARE), (0, PASS))
+        for t in range(PACK):
+            first_stage_pass(0, t, 0)
+        quantize_w1(0, 1, round_w1(0, 1, VECTOR_SHARE), (0, P, PASS))
+        for t in range(PACK):
+            first_stage_pass(0, t, 1)
+            apply_gain(0, t, t == 0)
+        for a in range(PASSES):
+            quantize_w1(1, a, round_w1(1, a, 0), (0, PASS))
+        for t in range(PACK):
+            for a in range(PASSES):
+                first_stage_pass(1, t, a)
+            apply_gain(1, t, False)
+
+        wa_raw = {}
+        for b in range(PASSES):
+            for u in range(2):
+                wa_raw[b, u] = raw_tile(WA_COLS)
+                nc.sync.dma_start(out=wa_raw[b, u][:], in_=pass_rows(wa, b)[:, :, u * WA_COLS : (u + 1) * WA_COLS])
+        nc.sync.dma_start(out=w4_w[:].bitcast(I32), in_=w4_words.rearrange("a p n -> p a n").bitcast(I32))
+        nc.sync.dma_start(out=read_t[1][:], in_=pass_rows(reading, 1))
+        for q in range(4):
+            nc.sync.dma_start(
+                out=w4_s[32 * q : 32 * q + 4, :, :].bitcast(I32),
+                in_=w4_scales[:, 4 * q : 4 * q + 4, :].rearrange("a r n -> r a n").bitcast(I32),
+            )
+
+        def quantize_wa(b, u):
+            rounded = slot_tile("cdfg"[2 * b + u], [P, WA_COLS, PACK], BF16)
+            nc.scalar.activation(
+                out=rounded[:].rearrange("p (c i) j -> p c j i", i=4),
+                in_=wa_raw[b, u][:].rearrange("p j (c i) -> p c j i", i=4),
+                func=COPY,
+            )
+            cols = slice(u * WA_COLS, (u + 1) * WA_COLS)
+            quantize(wa_w[b][:, cols], wa_s[b][:, cols], rounded[:].rearrange("p c j -> p (c j)"))
+
+        planes = {}
+        behind = {("lawn", 0, 0, 2): "c", ("edge", 0, 0, 2): "d"}
+        for t in range(PACK):
+            behind["edge", 1, 0, t] = "abce"[t]
+            behind["edge", 1, M_HALF, t] = "dfgh"[t]
+
+        def pick(kind, b, lo, hi, t):
+            if (kind, b, lo, t) in behind:
+                picked = slot_tile(behind[kind, b, lo, t], [P, hi - lo], F32)
+            else:
+                picked = ring.tile([P, hi - lo], F32, name="picked", tag="picked", bufs=3)
+            pos_t = pos1_t if kind == "edge" else pos2_t
+            nc.vector.tensor_copy(picked[:], h[b][t][:].indirect(pos_t[:, lo // 16 : hi // 16]))
+            return picked
+
+        def combine(kind, b, lo, hi, t, picked):
+            if t == 0:
+                planes[kind, b, lo] = ring.tile([P, PACK, hi - lo], BF16, name="planes", tag="planes_" + kind)
+            dst = planes[kind, b, lo][:, t, :]
+            if kind == "edge":
+                nc.vector.scalar_tensor_tensor(
+                    dst, picked[:], rim_t[:, b, t : t + 1], read_t[b][:, t, lo:hi], ALU.add, ALU.mult
+                )
+            else:
+                nc.vector.tensor_scalar_max(dst, picked[:], floor_t[:, b, t : t + 1])
+
+        def weave_and_quantize(kind, b, lo, hi, slot, copy=nc.scalar.copy):
+            woven = slot_tile(slot, [P, hi - lo, PACK], BF16)
+            copy(
+                out=woven[:].rearrange("p (c i) t -> p c t i", i=4),
+                in_=planes[kind, b, lo][:].rearrange("p t (c i) -> p c t i", i=4),
+            )
+            words, scales = (xa_w, xa_s) if kind == "edge" else (xb_w, xb_s)
+            quantize(words[b][:, lo:hi], scales[b][:, lo:hi], woven[:].rearrange("p m t -> p (m t)"))
+
+        def lawn_product():
+            for n in range(N_TILES):
+                yb = bank(6 + n % 2, [P, M])
+                for b in range(PASSES):
+                    nc.tensor.matmul_mx(
+                        out=yb[:],
+                        lhsT=w4_w[:, b, 2 * n * P : 2 * (n + 1) * P].bitcast(FP4X4),
+                        lhsT_scale=w4_s[:, b, n * P : (n + 1) * P],
+                        rhs=xb_w[b][:].bitcast(FP8X4),
+                        rhs_scale=xb_s[b][:],
+                        start=(b == 0),
+                        stop=(b == PASSES - 1),
+                    )
+                nc.scalar.activation(out=res[:, n, :], in_=yb[:], func=COPY, bias=1.0)
+
+        ya = {}
+
+        def edge_pass(b, half):
+            cols = slice(half * M_HALF, (half + 1) * M_HALF)
+            for pair in range(N_TILES // 2):
+                if b == 0:
+                    ya[half, pair] = bank(3 * half + pair, [P, 2, M_HALF])
+                for i in range(2):
+                    rows = slice((2 * pair + i) * P, (2 * pair + i + 1) * P)
+                    nc.tensor.matmul_mx(
+                        out=ya[half, pair][:, i, :],
+                        lhsT=wa_w[b][:, rows].bitcast(FP8X4),
+                        lhsT_scale=wa_s[b][:, rows],
+                        rhs=xa_w[b][:, cols].bitcast(FP8X4),
+                        rhs_scale=xa_s[b][:, cols],
+                        start=(b == 0 and i == 0),
+                        stop=(b == PASSES - 1 and i == 1),
+                    )
+
+        def finish(half):
+            cols = slice(half * M_HALF, (half + 1) * M_HALF)
+            for pair in range(N_TILES // 2):
+                part = res[:, 2 * pair : 2 * pair + 2, cols]
+                nc.vector.tensor_tensor(part, ya[half, pair][:], part, ALU.mult)
+                nc.sync.dma_start(
+                    out=out[2 * pair * P : (2 * pair + 2) * P, cols].rearrange("(i p) m -> p i m", p=P), in_=part
+                )
+
+        def after_first_group():
+            weave_and_quantize("lawn", 0, 0, M, "a")
+            weave_and_quantize("edge", 0, 0, M, "b")
+            quantize_wa(0, 0)
+
+        def after_lawn():
+            weave_and_quantize("lawn", 1, 0, M, "e")
+            quantize_wa(0, 1)
+            for half in range(2):
+                edge_pass(0, half)
+            lawn_product()
+            quantize_wa(1, 0)
+            quantize_wa(1, 1)
+
+        def after_edge(half):
+            if half == 0:
+                weave_and_quantize("edge", 1, 0, M_HALF, "h")
+            else:
+                weave_and_quantize("edge", 1, M_HALF, M, "a", nc.vector.tensor_copy)
+            edge_pass(1, half)
+
+        steps = [(kind, 0, 0, M, t) for t in range(PACK) for kind in ("lawn", "edge")]
+        steps = steps + [("lawn", 1, 0, M, t) for t in range(PACK)]
+        steps = steps + [("edge", 1, half * M_HALF, (half + 1) * M_HALF, t) for half in range(2) for t in range(PACK)]
+        then = {
+            ("edge", 0, 0): after_first_group,
+            ("lawn", 1, 0): after_lawn,
+            ("edge", 1, 0): lambda: after_edge(0),
+            ("edge", 1, M_HALF): lambda: after_edge(1),
+        }
+        picked = pick(*steps[0])
+        for step, following in zip(steps, steps[1:] + [None]):
+            ahead = pick(*following) if following else None
+            combine(*step, picked)
+            if step[4] == PACK - 1 and step[:3] in then:
+                then[step[:3]]()
+            picked = ahead
+        for half in range(2):
+            finish(half)

@@ -58,8 +58,8 @@ def tile_list_zone_edge_lawn_kernel(
         wa_s = [held.tile([P, N], U8, name="wa_s%d" % b, align_bytes=64) for b in range(PASSES)]
         w1_s = [[held.tile([P, PASS], U8, name="w1_s%d%d" % (b, a), align_bytes=64) for a in range(PASSES)]
                 for b in range(PASSES)]
-        h = [[held.tile([P, S], F32, name="h%d%d" % (b, t)) for t in range(PACK)] for b in range(PASSES)]
-        xb_w = [held.tile([P, M], U32, name="xb_w%d" % b, align_bytes=64) for b in range(PASSES)]
+        h = [[held.tile([P, S], F32, name="h0%d" % t) for t in range(PACK)]]
+        xb_w = [held.tile([P, M], U32, name="xb_w0", align_bytes=64), slot_tile("h", [P, M], U32)]
         xb_s = [held.tile([P, M], U8, name="xb_s%d" % b, align_bytes=64) for b in range(PASSES)]
         xa_w = [held.tile([P, M], U32, name="xa_w%d" % b, align_bytes=64) for b in range(PASSES)]
         xa_s = [held.tile([P, M], U8, name="xa_s%d" % b, align_bytes=64) for b in range(PASSES)]
@@ -77,28 +77,33 @@ def tile_list_zone_edge_lawn_kernel(
             return x[g * PASS : (g + 1) * PASS, :].rearrange("(p j) c -> p j c", j=PACK)
 
         nc.vector.memset(tab_s[:].bitcast(I32), 0)
-        nc.vector.memset(w4_s[:].rearrange("p a n -> p (a n)").bitcast(I32), 0)
-        for q in range(4):
-            nc.gpsimd.dma_start(
-                out=tab_s[32 * q : 32 * q + 8, :].bitcast(I32), in_=tab_scales[:, 4 * q : 4 * q + 4, :].bitcast(I32)
-            )
+        nc.gpsimd.memset(w4_s[:].rearrange("p a n -> p (a n)").bitcast(I32), 0)
+
         w1_raw = {}
 
-        def load_w1(b):
-            for a in range(PASSES):
-                w1_raw[b, a] = raw_tile(PASS)
-                nc.sync.dma_start(out=w1_raw[b, a][:], in_=pass_rows(w1, a)[:, :, b * PASS : (b + 1) * PASS])
+        def load_w1(b, a):
+            w1_raw[b, a] = raw_tile(PASS)
+            nc.sync.dma_start(out=w1_raw[b, a][:], in_=pass_rows(w1, a)[:, :, b * PASS : (b + 1) * PASS])
+
+        def load_table(a):
+            nc.sync.dma_start(out=tab_w[a][:], in_=tab_words[a].rearrange("p t i -> p (t i)").bitcast(I32))
 
         nc.sync.dma_start(offs_t[:], offs)
-        nc.sync.dma_start(out=tab_w[0][:], in_=tab_words[0].rearrange("p t i -> p (t i)").bitcast(I32))
+        load_table(0)
+        for q in range(4):
+            nc.sync.dma_start(
+                out=tab_s[32 * q : 32 * q + 8, :].bitcast(I32), in_=tab_scales[:, 4 * q : 4 * q + 4, :].bitcast(I32)
+            )
+        load_w1(0, 0)
+        load_table(1)
+        load_w1(0, 1)
         nc.sync.dma_start(pos2_t[:], pos2)
         nc.sync.dma_start(pos1_t[:], pos1)
         for vec_t, vec in ((gain_t, gain), (floor_t, floor_level), (rim_t, rim)):
             nc.sync.dma_start(out=vec_t[:], in_=vec.rearrange("(b p t) -> p b t", b=PASSES, t=PACK))
-        nc.sync.dma_start(out=tab_w[1][:], in_=tab_words[1].rearrange("p t i -> p (t i)").bitcast(I32))
-        load_w1(0)
         nc.sync.dma_start(out=read_t[0][:], in_=pass_rows(reading, 0))
-        load_w1(1)
+        for a in range(PASSES):
+            load_w1(1, a)
 
         nc.vector.tensor_copy(v_s[:], tab_s[:].indirect(offs_t[:]))
         v_w = [held.tile([P, S], U32, name="v_w0", align_bytes=64), slot_tile("table", [P, S], U32)]
@@ -121,16 +126,13 @@ def tile_list_zone_edge_lawn_kernel(
             for lo, hi in zip(edges, edges[1:]):
                 quantize(w1_w[b][a][:, lo:hi], w1_s[b][a][:, lo:hi], rounded[:, PACK * lo : PACK * hi])
 
-        acc = {}
-
-        def first_stage_pass(b, t, a):
+        def first_stage(b, t, half):
             rows = slice(t * P, (t + 1) * P)
-            for half in range(2):
-                if a == 0:
-                    acc[b, t, half] = bank(2 * t + half, [P, BANK])
-                cols = slice(half * BANK, (half + 1) * BANK)
+            cols = slice(half * BANK, (half + 1) * BANK)
+            acc = bank(2 * t + half, [P, BANK])
+            for a in range(PASSES):
                 nc.tensor.matmul_mx(
-                    out=acc[b, t, half][:],
+                    out=acc[:],
                     lhsT=w1_w[b][a][:, rows].bitcast(FP8X4),
                     lhsT_scale=w1_s[b][a][:, rows],
                     rhs=v_w[a][:, cols].bitcast(FP8X4),
@@ -138,28 +140,19 @@ def tile_list_zone_edge_lawn_kernel(
                     start=(a == 0),
                     stop=(a == PASSES - 1),
                 )
-
-        def apply_gain(b, t, vector_helps):
             g = gain_t[:, b, t : t + 1]
-            nc.scalar.activation(out=h[b][t][:, :BANK], in_=acc[b, t, 0][:], func=COPY, scale=g)
-            if vector_helps:
-                nc.vector.tensor_scalar_mul(h[b][t][:, BANK:], acc[b, t, 1][:], g)
+            if (b, t, half) == (0, 0, 1):
+                nc.vector.tensor_scalar_mul(h[b][t][:, cols], acc[:], g)
             else:
-                nc.scalar.activation(out=h[b][t][:, BANK:], in_=acc[b, t, 1][:], func=COPY, scale=g)
+                nc.scalar.activation(out=h[b][t][:, cols], in_=acc[:], func=COPY, scale=g)
 
-        quantize_w1(0, 0, round_w1(0, 0, VECTOR_SHARE), (0, PASS))
-        for t in range(PACK):
-            first_stage_pass(0, t, 0)
+        quantize_w1(0, 0, round_w1(0, 0, 0), (0, PASS))
         quantize_w1(0, 1, round_w1(0, 1, VECTOR_SHARE), (0, P, PASS))
         for t in range(PACK):
-            first_stage_pass(0, t, 1)
-            apply_gain(0, t, t == 0)
+            for half in range(2):
+                first_stage(0, t, half)
         for a in range(PASSES):
             quantize_w1(1, a, round_w1(1, a, 0), (0, PASS))
-        for t in range(PACK):
-            for a in range(PASSES):
-                first_stage_pass(1, t, a)
-            apply_gain(1, t, False)
 
         wa_raw = {}
         for b in range(PASSES):
@@ -175,7 +168,7 @@ def tile_list_zone_edge_lawn_kernel(
             )
 
         def quantize_wa(b, u):
-            rounded = slot_tile("cdfg"[2 * b + u], [P, WA_COLS, PACK], BF16)
+            rounded = slot_tile("fg"[u], [P, WA_COLS, PACK], BF16)
             nc.scalar.activation(
                 out=rounded[:].rearrange("p (c i) j -> p c j i", i=4),
                 in_=wa_raw[b, u][:].rearrange("p j (c i) -> p c j i", i=4),
@@ -185,18 +178,29 @@ def tile_list_zone_edge_lawn_kernel(
             quantize(wa_w[b][:, cols], wa_s[b][:, cols], rounded[:].rearrange("p c j -> p (c j)"))
 
         planes = {}
-        behind = {("lawn", 0, 0, 2): "c", ("edge", 0, 0, 2): "d"}
-        for t in range(PACK):
-            behind["edge", 1, 0, t] = "abce"[t]
-            behind["edge", 1, M_HALF, t] = "dfgh"[t]
+        def behind(slot, count, width):
+            group = slot_tile(slot, [P, count, width], F32)
+            return [group[:, i, :] for i in range(count)]
+
+        held_back = {
+            ("lawn", 0, 0, 2): ("c", 2),
+            ("edge", 0, 0, 2): ("d", 2),
+            ("edge", 1, 0, 0): ("b", 4),
+            ("edge", 1, M_HALF, 0): ("g", 4),
+        }
+        places = {}
 
         def pick(kind, b, lo, hi, t):
-            if (kind, b, lo, t) in behind:
-                picked = slot_tile(behind[kind, b, lo, t], [P, hi - lo], F32)
+            if (kind, b, lo, t) in held_back:
+                slot, count = held_back[kind, b, lo, t]
+                for i, place in enumerate(behind(slot, count, hi - lo)):
+                    places[kind, b, lo, t + i] = place
+            if (kind, b, lo, t) in places:
+                picked = places[kind, b, lo, t]
             else:
-                picked = ring.tile([P, hi - lo], F32, name="picked", tag="picked", bufs=3)
+                picked = ring.tile([P, hi - lo], F32, name="picked", tag="picked", bufs=3)[:]
             pos_t = pos1_t if kind == "edge" else pos2_t
-            nc.vector.tensor_copy(picked[:], h[b][t][:].indirect(pos_t[:, lo // 16 : hi // 16]))
+            nc.vector.tensor_copy(picked, h[b][t][:].indirect(pos_t[:, lo // 16 : hi // 16]))
             return picked
 
         def combine(kind, b, lo, hi, t, picked):
@@ -205,10 +209,10 @@ def tile_list_zone_edge_lawn_kernel(
             dst = planes[kind, b, lo][:, t, :]
             if kind == "edge":
                 nc.vector.scalar_tensor_tensor(
-                    dst, picked[:], rim_t[:, b, t : t + 1], read_t[b][:, t, lo:hi], ALU.add, ALU.mult
+                    dst, picked, rim_t[:, b, t : t + 1], read_t[b][:, t, lo:hi], ALU.add, ALU.mult
                 )
             else:
-                nc.vector.tensor_scalar_max(dst, picked[:], floor_t[:, b, t : t + 1])
+                nc.vector.tensor_scalar_max(dst, picked, floor_t[:, b, t : t + 1])
 
         def weave_and_quantize(kind, b, lo, hi, slot, copy=nc.scalar.copy):
             woven = slot_tile(slot, [P, hi - lo, PACK], BF16)
@@ -265,25 +269,33 @@ def tile_list_zone_edge_lawn_kernel(
         def after_first_group():
             weave_and_quantize("lawn", 0, 0, M, "a")
             weave_and_quantize("edge", 0, 0, M, "b")
-            quantize_wa(0, 0)
+            for half in range(2):
+                edge_pass(0, half)
 
         def after_lawn():
             weave_and_quantize("lawn", 1, 0, M, "e")
-            quantize_wa(0, 1)
-            for half in range(2):
-                edge_pass(0, half)
+            for u in range(2):
+                quantize_wa(1, u)
             lawn_product()
-            quantize_wa(1, 0)
-            quantize_wa(1, 1)
 
         def after_edge(half):
             if half == 0:
                 weave_and_quantize("edge", 1, 0, M_HALF, "h")
             else:
-                weave_and_quantize("edge", 1, M_HALF, M, "a", nc.vector.tensor_copy)
+                weave_and_quantize("edge", 1, M_HALF, M, "h", nc.vector.tensor_copy)
             edge_pass(1, half)
 
-        steps = [(kind, 0, 0, M, t) for t in range(PACK) for kind in ("lawn", "edge")]
+        for u in range(2):
+            quantize_wa(0, u)
+        h.append(
+            [ring.tile([P, S], F32, name="h_on_raw", tag="raw", bufs=4) for t in range(2)]
+            + [held.tile([P, S], F32, name="h1%d" % t) for t in range(2, PACK)]
+        )
+        for half in range(2):
+            for t in range(PACK):
+                first_stage(1, t, half)
+        steps = [(kind, 0, 0, M, t) for t in range(2) for kind in ("lawn", "edge")]
+        steps = steps + [(kind, 0, 0, M, t) for kind in ("lawn", "edge") for t in range(2, PACK)]
         steps = steps + [("lawn", 1, 0, M, t) for t in range(PACK)]
         steps = steps + [("edge", 1, half * M_HALF, (half + 1) * M_HALF, t) for half in range(2) for t in range(PACK)]
         then = {

@@ -45,12 +45,12 @@ def tile_list_zone_edge_lawn_kernel(
         offs_t = held.tile([P, S // 16], U16, name="offs_t")
         pos1_t = held.tile([P, M // 16], U16, name="pos1_t")
         pos2_t = held.tile([P, M // 16], U16, name="pos2_t")
-        tab_w = [held.tile([P, T], I32, name="tab_w%d" % a) for a in range(PASSES)]
+        tab_w = [slot_tile("words%d" % a, [P, T], I32) for a in range(PASSES)]
         tab_s = slot_tile("table", [P, T], U8)
         v_s = held.tile([P, S], U8, name="v_s", align_bytes=64)
-        gain_t = held.tile([P, PASSES, PACK], F32, name="gain_t")
-        rim_t = held.tile([P, PASSES, PACK], F32, name="rim_t")
-        floor_t = held.tile([P, PASSES, PACK], F32, name="floor_t")
+        gain_t = held.tile([P, PASSES, 2 * PACK], F32, name="gain_t")
+        rim_t = held.tile([P, PASSES, 2 * PACK], F32, name="rim_t")
+        floor_t = held.tile([P, PASSES, 2 * PACK], F32, name="floor_t")
         read_t = [held.tile([P, PACK, M], F32, name="read_t%d" % b) for b in range(PASSES)]
         w4_w = held.tile([P, PASSES, 2 * N], U8, name="w4_w", align_bytes=64)
         w4_s = held.tile([P, PASSES, N], U8, name="w4_s", align_bytes=64)
@@ -58,7 +58,7 @@ def tile_list_zone_edge_lawn_kernel(
         wa_s = [held.tile([P, N], U8, name="wa_s%d" % b, align_bytes=64) for b in range(PASSES)]
         w1_s = [[held.tile([P, PASS], U8, name="w1_s%d%d" % (b, a), align_bytes=64) for a in range(PASSES)]
                 for b in range(PASSES)]
-        h = [[held.tile([P, S], F32, name="h0%d" % t) for t in range(PACK)]]
+        h = [[held.tile([P, S], F32, name="h%d%d" % (b, t)) for t in range(PACK)] for b in range(PASSES)]
         xb_w = [held.tile([P, M], U32, name="xb_w0", align_bytes=64), slot_tile("h", [P, M], U32)]
         xb_s = [held.tile([P, M], U8, name="xb_s%d" % b, align_bytes=64) for b in range(PASSES)]
         xa_w = [held.tile([P, M], U32, name="xa_w%d" % b, align_bytes=64) for b in range(PASSES)]
@@ -76,8 +76,8 @@ def tile_list_zone_edge_lawn_kernel(
         def pass_rows(x, g):
             return x[g * PASS : (g + 1) * PASS, :].rearrange("(p j) c -> p j c", j=PACK)
 
-        nc.vector.memset(tab_s[:].bitcast(I32), 0)
-        nc.gpsimd.memset(w4_s[:].rearrange("p a n -> p (a n)").bitcast(I32), 0)
+        nc.gpsimd.memset(tab_s[:].bitcast(I32), 0)
+        nc.vector.memset(w4_s[:].rearrange("p a n -> p (a n)").bitcast(I32), 0)
 
         w1_raw = {}
 
@@ -88,19 +88,23 @@ def tile_list_zone_edge_lawn_kernel(
         def load_table(a):
             nc.sync.dma_start(out=tab_w[a][:], in_=tab_words[a].rearrange("p t i -> p (t i)").bitcast(I32))
 
+        def load_vector(vec_t, vec):
+            nc.sync.dma_start(out=vec_t[:, :, :PACK], in_=vec.rearrange("(b p t) -> p b t", b=PASSES, t=PACK))
+
         nc.sync.dma_start(offs_t[:], offs)
         load_table(0)
         for q in range(4):
-            nc.sync.dma_start(
+            nc.gpsimd.dma_start(
                 out=tab_s[32 * q : 32 * q + 8, :].bitcast(I32), in_=tab_scales[:, 4 * q : 4 * q + 4, :].bitcast(I32)
             )
         load_w1(0, 0)
         load_table(1)
         load_w1(0, 1)
+        load_vector(gain_t, gain)
         nc.sync.dma_start(pos2_t[:], pos2)
+        load_vector(floor_t, floor_level)
         nc.sync.dma_start(pos1_t[:], pos1)
-        for vec_t, vec in ((gain_t, gain), (floor_t, floor_level), (rim_t, rim)):
-            nc.sync.dma_start(out=vec_t[:], in_=vec.rearrange("(b p t) -> p b t", b=PASSES, t=PACK))
+        load_vector(rim_t, rim)
         nc.sync.dma_start(out=read_t[0][:], in_=pass_rows(reading, 0))
         for a in range(PASSES):
             load_w1(1, a)
@@ -153,12 +157,14 @@ def tile_list_zone_edge_lawn_kernel(
                 first_stage(0, t, half)
         for a in range(PASSES):
             quantize_w1(1, a, round_w1(1, a, 0), (0, PASS))
+        for t in range(PACK):
+            for half in range(2):
+                first_stage(1, t, half)
 
         wa_raw = {}
         for b in range(PASSES):
-            for u in range(2):
-                wa_raw[b, u] = raw_tile(WA_COLS)
-                nc.sync.dma_start(out=wa_raw[b, u][:], in_=pass_rows(wa, b)[:, :, u * WA_COLS : (u + 1) * WA_COLS])
+            wa_raw[b] = slot_tile("words%d" % b, [P, PACK, N], F32)
+            nc.sync.dma_start(out=wa_raw[b][:], in_=pass_rows(wa, b))
         nc.sync.dma_start(out=w4_w[:].bitcast(I32), in_=w4_words.rearrange("a p n -> p a n").bitcast(I32))
         nc.sync.dma_start(out=read_t[1][:], in_=pass_rows(reading, 1))
         for q in range(4):
@@ -169,32 +175,32 @@ def tile_list_zone_edge_lawn_kernel(
 
         def quantize_wa(b, u):
             rounded = slot_tile("fg"[u], [P, WA_COLS, PACK], BF16)
+            cols = slice(u * WA_COLS, (u + 1) * WA_COLS)
             nc.scalar.activation(
                 out=rounded[:].rearrange("p (c i) j -> p c j i", i=4),
-                in_=wa_raw[b, u][:].rearrange("p j (c i) -> p c j i", i=4),
+                in_=wa_raw[b][:, :, cols].rearrange("p j (c i) -> p c j i", i=4),
                 func=COPY,
             )
-            cols = slice(u * WA_COLS, (u + 1) * WA_COLS)
             quantize(wa_w[b][:, cols], wa_s[b][:, cols], rounded[:].rearrange("p c j -> p (c j)"))
 
         planes = {}
-        def behind(slot, count, width):
-            group = slot_tile(slot, [P, count, width], F32)
-            return [group[:, i, :] for i in range(count)]
-
         held_back = {
-            ("lawn", 0, 0, 2): ("c", 2),
-            ("edge", 0, 0, 2): ("d", 2),
-            ("edge", 1, 0, 0): ("b", 4),
-            ("edge", 1, M_HALF, 0): ("g", 4),
+            "c": [("lawn", 0, 0, 2)],
+            "d": [("lawn", 0, 0, 3), ("edge", 0, 0, 2), ("edge", 0, 0, 3)],
+            "lawn": [("lawn", 1, 0, t) for t in range(PACK)],
+            "b": [("edge", 1, 0, t) for t in range(PACK)],
+            "f": [("edge", 1, M_HALF, t) for t in range(PACK)],
         }
         places = {}
+        groups = {}
 
         def pick(kind, b, lo, hi, t):
-            if (kind, b, lo, t) in held_back:
-                slot, count = held_back[kind, b, lo, t]
-                for i, place in enumerate(behind(slot, count, hi - lo)):
-                    places[kind, b, lo, t + i] = place
+            for slot, group in held_back.items():
+                if group[0] == (kind, b, lo, t):
+                    shared = slot_tile(slot, [P, len(group), hi - lo], F32)
+                    groups[slot] = shared
+                    for i, member in enumerate(group):
+                        places[member] = shared[:, i, :]
             if (kind, b, lo, t) in places:
                 picked = places[kind, b, lo, t]
             else:
@@ -204,6 +210,8 @@ def tile_list_zone_edge_lawn_kernel(
             return picked
 
         def combine(kind, b, lo, hi, t, picked):
+            if (kind, b) == ("lawn", 1):
+                return
             if t == 0:
                 planes[kind, b, lo] = ring.tile([P, PACK, hi - lo], BF16, name="planes", tag="planes_" + kind)
             dst = planes[kind, b, lo][:, t, :]
@@ -225,7 +233,7 @@ def tile_list_zone_edge_lawn_kernel(
 
         def lawn_product():
             for n in range(N_TILES):
-                yb = bank(6 + n % 2, [P, M])
+                yb = bank(n, [P, M])
                 for b in range(PASSES):
                     nc.tensor.matmul_mx(
                         out=yb[:],
@@ -257,26 +265,30 @@ def tile_list_zone_edge_lawn_kernel(
                         stop=(b == PASSES - 1 and i == 1),
                     )
 
-        def finish(half):
+        def finish(half, lo, hi):
             cols = slice(half * M_HALF, (half + 1) * M_HALF)
-            for pair in range(N_TILES // 2):
-                part = res[:, 2 * pair : 2 * pair + 2, cols]
-                nc.vector.tensor_tensor(part, ya[half, pair][:], part, ALU.mult)
-                nc.sync.dma_start(
-                    out=out[2 * pair * P : (2 * pair + 2) * P, cols].rearrange("(i p) m -> p i m", p=P), in_=part
-                )
+            part = res[:, lo:hi, cols]
+            nc.vector.tensor_tensor(part, ya[half, lo // 2][:, lo % 2 : lo % 2 + hi - lo, :], part, ALU.mult)
+            nc.sync.dma_start(out=out[lo * P : hi * P, cols].rearrange("(i p) m -> p i m", p=P), in_=part)
 
         def after_first_group():
             weave_and_quantize("lawn", 0, 0, M, "a")
             weave_and_quantize("edge", 0, 0, M, "b")
-            for half in range(2):
-                edge_pass(0, half)
 
         def after_lawn():
-            weave_and_quantize("lawn", 1, 0, M, "e")
+            woven = slot_tile("e", [P, M, PACK], BF16)
+            nc.vector.tensor_tensor(
+                woven[:].rearrange("p (c i) t -> p c t i", i=2),
+                groups["lawn"][:].rearrange("p t (c i) -> p c t i", i=2),
+                floor_t[:, 1, :PACK].unsqueeze(1).unsqueeze(3).to_broadcast([P, M // 2, PACK, 2]),
+                ALU.max,
+            )
+            quantize(xb_w[1][:], xb_s[1][:], woven[:].rearrange("p m t -> p (m t)"))
             for u in range(2):
                 quantize_wa(1, u)
             lawn_product()
+            for half in range(2):
+                edge_pass(0, half)
 
         def after_edge(half):
             if half == 0:
@@ -287,13 +299,6 @@ def tile_list_zone_edge_lawn_kernel(
 
         for u in range(2):
             quantize_wa(0, u)
-        h.append(
-            [ring.tile([P, S], F32, name="h_on_raw", tag="raw", bufs=4) for t in range(2)]
-            + [held.tile([P, S], F32, name="h1%d" % t) for t in range(2, PACK)]
-        )
-        for half in range(2):
-            for t in range(PACK):
-                first_stage(1, t, half)
         steps = [(kind, 0, 0, M, t) for t in range(2) for kind in ("lawn", "edge")]
         steps = steps + [(kind, 0, 0, M, t) for kind in ("lawn", "edge") for t in range(2, PACK)]
         steps = steps + [("lawn", 1, 0, M, t) for t in range(PACK)]
@@ -311,5 +316,6 @@ def tile_list_zone_edge_lawn_kernel(
             if step[4] == PACK - 1 and step[:3] in then:
                 then[step[:3]]()
             picked = ahead
-        for half in range(2):
-            finish(half)
+        for half, edges in enumerate(((0, 2, 4, 6), (0, 2, 4, 6))):
+            for lo, hi in zip(edges, edges[1:]):
+                finish(half, lo, hi)

@@ -24,7 +24,7 @@ PASSES = 2
 N_TILES = N // P
 WA_COLS = N // 2
 M_HALF = M // 2
-VECTOR_SHARE = 80
+VECTOR_SHARE = 40
 
 
 def tile_list_zone_edge_lawn_kernel(
@@ -88,8 +88,8 @@ def tile_list_zone_edge_lawn_kernel(
         def load_table(a):
             nc.sync.dma_start(out=tab_w[a][:], in_=tab_words[a].rearrange("p t i -> p (t i)").bitcast(I32))
 
-        def load_vector(vec_t, vec):
-            nc.sync.dma_start(out=vec_t[:, :, :PACK], in_=vec.rearrange("(b p t) -> p b t", b=PASSES, t=PACK))
+        def load_vector(vec_t, vec, b):
+            nc.sync.dma_start(out=vec_t[:, b, :PACK], in_=vec.rearrange("(b p t) -> p b t", b=PASSES, t=PACK)[:, b, :])
 
         nc.sync.dma_start(offs_t[:], offs)
         load_table(0)
@@ -100,14 +100,16 @@ def tile_list_zone_edge_lawn_kernel(
         load_w1(0, 0)
         load_table(1)
         load_w1(0, 1)
-        load_vector(gain_t, gain)
+        load_vector(gain_t, gain, 0)
         nc.sync.dma_start(pos2_t[:], pos2)
-        load_vector(floor_t, floor_level)
+        load_vector(floor_t, floor_level, 0)
         nc.sync.dma_start(pos1_t[:], pos1)
-        load_vector(rim_t, rim)
+        load_vector(rim_t, rim, 0)
         nc.sync.dma_start(out=read_t[0][:], in_=pass_rows(reading, 0))
         for a in range(PASSES):
             load_w1(1, a)
+        for vec_t, vec in ((gain_t, gain), (floor_t, floor_level), (rim_t, rim)):
+            load_vector(vec_t, vec, 1)
 
         nc.vector.tensor_copy(v_s[:], tab_s[:].indirect(offs_t[:]))
         v_w = [held.tile([P, S], U32, name="v_w0", align_bytes=64), slot_tile("table", [P, S], U32)]
@@ -116,11 +118,15 @@ def tile_list_zone_edge_lawn_kernel(
 
         def round_w1(b, a, vector_share):
             rounded = slot_tile({(0, 0): "d", (0, 1): "e", (1, 0): "c", (1, 1): "d"}[b, a], [P, PACK, P, PACK], BF16)
-            dst = rounded[:].rearrange("p t m j -> p m j t")
-            src = w1_raw[b, a][:].rearrange("p j (m t) -> p m j t", t=PACK)
+            dst = rounded[:].rearrange("p t (m i) j -> p m j i t", i=2)
+            src = w1_raw[b, a][:].rearrange("p j (m i t) -> p m j i t", i=2, t=PACK)
             if vector_share:
                 nc.vector.tensor_copy(out=dst[:, :vector_share], in_=src[:, :vector_share])
-            nc.scalar.activation(out=dst[:, vector_share:], in_=src[:, vector_share:], func=COPY)
+            first = vector_share
+            if (b, a) == (0, 0):
+                nc.scalar.activation(out=dst[:, 0], in_=src[:, 0], func=COPY)
+                first = 1
+            nc.scalar.copy(out=dst[:, first:], in_=src[:, first:])
             return rounded[:].rearrange("p t m j -> p (t m j)")
 
         def quantize(words, scales, values):

@@ -24,7 +24,7 @@ PASSES = 2
 N_TILES = N // P
 WA_COLS = N // 2
 M_HALF = M // 2
-VECTOR_SHARE = 40
+VECTOR_SHARE = 18
 
 
 def tile_list_zone_edge_lawn_kernel(
@@ -81,9 +81,13 @@ def tile_list_zone_edge_lawn_kernel(
 
         w1_raw = {}
 
-        def load_w1(b, a):
-            w1_raw[b, a] = raw_tile(PASS)
-            nc.sync.dma_start(out=w1_raw[b, a][:], in_=pass_rows(w1, a)[:, :, b * PASS : (b + 1) * PASS])
+        def load_w1(b, a, parts=1):
+            width = PASS // parts
+            w1_raw[b, a] = []
+            for lo in range(b * PASS, (b + 1) * PASS, width):
+                raw = raw_tile(width)
+                nc.sync.dma_start(out=raw[:], in_=pass_rows(w1, a)[:, :, lo : lo + width])
+                w1_raw[b, a].append(raw)
 
         def load_table(a):
             nc.sync.dma_start(out=tab_w[a][:], in_=tab_words[a].rearrange("p t i -> p (t i)").bitcast(I32))
@@ -99,7 +103,7 @@ def tile_list_zone_edge_lawn_kernel(
             )
         load_w1(0, 0)
         load_table(1)
-        load_w1(0, 1)
+        load_w1(0, 1, 2)
         load_vector(gain_t, gain, 0)
         nc.sync.dma_start(pos2_t[:], pos2)
         load_vector(floor_t, floor_level, 0)
@@ -118,15 +122,19 @@ def tile_list_zone_edge_lawn_kernel(
 
         def round_w1(b, a, vector_share):
             rounded = slot_tile({(0, 0): "d", (0, 1): "e", (1, 0): "c", (1, 1): "d"}[b, a], [P, PACK, P, PACK], BF16)
-            dst = rounded[:].rearrange("p t (m i) j -> p m j i t", i=2)
-            src = w1_raw[b, a][:].rearrange("p j (m i t) -> p m j i t", i=2, t=PACK)
-            if vector_share:
-                nc.vector.tensor_copy(out=dst[:, :vector_share], in_=src[:, :vector_share])
-            first = vector_share
-            if (b, a) == (0, 0):
-                nc.scalar.activation(out=dst[:, 0], in_=src[:, 0], func=COPY)
-                first = 1
-            nc.scalar.copy(out=dst[:, first:], in_=src[:, first:])
+            pairs = rounded[:].rearrange("p t (m i) j -> p m j i t", i=2)
+            parts = w1_raw[b, a]
+            width = P // 2 // len(parts)
+            for n, raw in enumerate(parts):
+                dst = pairs[:, n * width : (n + 1) * width]
+                src = raw[:].rearrange("p j (m i t) -> p m j i t", i=2, t=PACK)
+                first = vector_share if raw is parts[-1] else 0
+                if first:
+                    nc.vector.tensor_copy(out=dst[:, :first], in_=src[:, :first])
+                if (b, a) == (0, 0):
+                    nc.scalar.activation(out=dst[:, 0], in_=src[:, 0], func=COPY)
+                    first = 1
+                nc.scalar.copy(out=dst[:, first:], in_=src[:, first:])
             return rounded[:].rearrange("p t m j -> p (t m j)")
 
         def quantize(words, scales, values):
@@ -194,7 +202,8 @@ def tile_list_zone_edge_lawn_kernel(
             "c": [("lawn", 0, 0, 2)],
             "d": [("lawn", 0, 0, 3), ("edge", 0, 0, 2), ("edge", 0, 0, 3)],
             "lawn": [("lawn", 1, 0, t) for t in range(PACK)],
-            "b": [("edge", 1, 0, t) for t in range(PACK)],
+            "b": [("edge", 1, 0, t) for t in range(2)],
+            "e": [("edge", 1, 0, t) for t in range(2, PACK)],
             "f": [("edge", 1, M_HALF, t) for t in range(PACK)],
         }
         places = {}
@@ -216,8 +225,6 @@ def tile_list_zone_edge_lawn_kernel(
             return picked
 
         def combine(kind, b, lo, hi, t, picked):
-            if (kind, b) == ("lawn", 1):
-                return
             if t == 0:
                 planes[kind, b, lo] = ring.tile([P, PACK, hi - lo], BF16, name="planes", tag="planes_" + kind)
             dst = planes[kind, b, lo][:, t, :]
@@ -282,14 +289,7 @@ def tile_list_zone_edge_lawn_kernel(
             weave_and_quantize("edge", 0, 0, M, "b")
 
         def after_lawn():
-            woven = slot_tile("e", [P, M, PACK], BF16)
-            nc.vector.tensor_tensor(
-                woven[:].rearrange("p (c i) t -> p c t i", i=2),
-                groups["lawn"][:].rearrange("p t (c i) -> p c t i", i=2),
-                floor_t[:, 1, :PACK].unsqueeze(1).unsqueeze(3).to_broadcast([P, M // 2, PACK, 2]),
-                ALU.max,
-            )
-            quantize(xb_w[1][:], xb_s[1][:], woven[:].rearrange("p m t -> p (m t)"))
+            weave_and_quantize("lawn", 1, 0, M, "e")
             for u in range(2):
                 quantize_wa(1, u)
             lawn_product()

from contextlib import ExitStack

import concourse.mybir as mybir

K, T, S, H, M, N = 1024, 4096, 1024, 1024, 512, 768
FLOPS = 2 * K * H * S + 2 * 2 * H * N * M

F32 = mybir.dt.float32
BF16 = mybir.dt.bfloat16
I32 = mybir.dt.int32
U32 = mybir.dt.uint32
U16 = mybir.dt.uint16
U8 = mybir.dt.uint8
FP8X4 = mybir.dt.float8_e4m3fn_x4
FP4X4 = mybir.dt.float4_e2m1fn_x4
ALU = mybir.AluOpType
COPY = mybir.ActivationFunctionType.Copy

P = 128
PACK = 4
PASS = P * PACK
BANK = 512
PASSES = 2
N_TILES = N // P
WA_COLS = N // 2
M_HALF = M // 2
VECTOR_SHARE = 18


def tile_list_zone_edge_lawn_kernel(
    tc, tab_words, tab_scales, offs, pos1, pos2, w1, gain, rim, reading, floor_level, wa, w4_words, w4_scales, out
):
    nc = tc.nc
    with ExitStack() as ctx:
        held = ctx.enter_context(tc.tile_pool(name="held", bufs=1))
        ring = ctx.enter_context(tc.tile_pool(name="ring", bufs=2))
        psum = ctx.enter_context(tc.psum_pool(name="psum", bufs=1))

        def bank(i, shape):
            return psum.tile(shape, F32, name="bank%d" % i, tag="bank%d" % i)

        def slot_tile(slot, shape, dtype):
            return held.tile(shape, dtype, name="slot_%s" % slot, tag="slot_%s" % slot, align_bytes=64)

        offs_t = held.tile([P, S // 16], U16, name="offs_t")
        pos1_t = held.tile([P, M // 16], U16, name="pos1_t")
        pos2_t = held.tile([P, M // 16], U16, name="pos2_t")
        tab_w = [slot_tile("words%d" % a, [P, T], I32) for a in range(PASSES)]
        tab_s = slot_tile("table", [P, T], U8)
        v_s = held.tile([P, S], U8, name="v_s", align_bytes=64)
        gain_t = held.tile([P, PASSES, 2 * PACK], F32, name="gain_t")
        rim_t = held.tile([P, PASSES, 2 * PACK], F32, name="rim_t")
        floor_t = held.tile([P, PASSES, 2 * PACK], F32, name="floor_t")
        read_t = [held.tile([P, PACK, M], F32, name="read_t%d" % b) for b in range(PASSES)]
        w4_w = held.tile([P, PASSES, 2 * N], U8, name="w4_w", align_bytes=64)
        w4_s = held.tile([P, PASSES, N], U8, name="w4_s", align_bytes=64)
        wa_w = [held.tile([P, N], U32, name="wa_w%d" % b, align_bytes=64) for b in range(PASSES)]
        wa_s = [held.tile([P, N], U8, name="wa_s%d" % b, align_bytes=64) for b in range(PASSES)]
        w1_s = [[held.tile([P, PASS], U8, name="w1_s%d%d" % (b, a), align_bytes=64) for a in range(PASSES)]
                for b in range(PASSES)]
        h = [[held.tile([P, S], F32, name="h%d%d" % (b, t)) for t in range(PACK)] for b in range(PASSES)]
        xb_w = [held.tile([P, M], U32, name="xb_w0", align_bytes=64), slot_tile("h", [P, M], U32)]
        xb_s = [held.tile([P, M], U8, name="xb_s%d" % b, align_bytes=64) for b in range(PASSES)]
        xa_w = [held.tile([P, M], U32, name="xa_w%d" % b, align_bytes=64) for b in range(PASSES)]
        xa_s = [held.tile([P, M], U8, name="xa_s%d" % b, align_bytes=64) for b in range(PASSES)]
        res = held.tile([P, N_TILES, M], F32, name="res")

        w1_w = [
            [held.tile([P, PASS], U32, name="w1_w00", align_bytes=64), slot_tile("c", [P, PASS], U32)],
            [slot_tile("a", [P, PASS], U32), slot_tile("b", [P, PASS], U32)],
        ]

        def raw_tile(cols):
            return ring.tile([P, PACK, cols], F32, name="raw", tag="raw", bufs=4)

        def pass_rows(x, g):
            return x[g * PASS : (g + 1) * PASS, :].rearrange("(p j) c -> p j c", j=PACK)

        nc.gpsimd.memset(tab_s[:].bitcast(I32), 0)
        nc.vector.memset(w4_s[:].rearrange("p a n -> p (a n)").bitcast(I32), 0)

        w1_raw = {}

        def load_w1(b, a, parts=1):
            width = PASS // parts
            w1_raw[b, a] = []
            for lo in range(b * PASS, (b + 1) * PASS, width):
                raw = raw_tile(width)
                nc.sync.dma_start(out=raw[:], in_=pass_rows(w1, a)[:, :, lo : lo + width])
                w1_raw[b, a].append(raw)

        def load_table(a):
            nc.sync.dma_start(out=tab_w[a][:], in_=tab_words[a].rearrange("p t i -> p (t i)").bitcast(I32))

        def load_vector(vec_t, vec, b):
            nc.sync.dma_start(out=vec_t[:, b, :PACK], in_=vec.rearrange("(b p t) -> p b t", b=PASSES, t=PACK)[:, b, :])

        nc.sync.dma_start(offs_t[:], offs)
        load_table(0)
        for q in range(4):
            nc.gpsimd.dma_start(
                out=tab_s[32 * q : 32 * q + 8, :].bitcast(I32), in_=tab_scales[:, 4 * q : 4 * q + 4, :].bitcast(I32)
            )
        load_w1(0, 0)
        load_table(1)
        load_w1(0, 1, 2)
        load_vector(gain_t, gain, 0)
        nc.sync.dma_start(pos2_t[:], pos2)
        load_vector(floor_t, floor_level, 0)
        nc.sync.dma_start(pos1_t[:], pos1)
        load_vector(rim_t, rim, 0)
        nc.sync.dma_start(out=read_t[0][:], in_=pass_rows(reading, 0))
        for a in range(PASSES):
            load_w1(1, a)
        for vec_t, vec in ((gain_t, gain), (floor_t, floor_level), (rim_t, rim)):
            load_vector(vec_t, vec, 1)

        nc.vector.tensor_copy(v_s[:], tab_s[:].indirect(offs_t[:]))
        v_w = [held.tile([P, S], U32, name="v_w0", align_bytes=64), slot_tile("table", [P, S], U32)]
        for a in range(PASSES):
            nc.vector.tensor_copy(v_w[a][:], tab_w[a][:].bitcast(U32).indirect(offs_t[:]))

        def round_w1(b, a, vector_share):
            rounded = slot_tile({(0, 0): "d", (0, 1): "e", (1, 0): "c", (1, 1): "d"}[b, a], [P, PACK, P, PACK], BF16)
            pairs = rounded[:].rearrange("p t (m i) j -> p m j i t", i=2)
            parts = w1_raw[b, a]
            width = P // 2 // len(parts)
            for n, raw in enumerate(parts):
                dst = pairs[:, n * width : (n + 1) * width]
                src = raw[:].rearrange("p j (m i t) -> p m j i t", i=2, t=PACK)
                first = vector_share if raw is parts[-1] else 0
                if first:
                    nc.vector.tensor_copy(out=dst[:, :first], in_=src[:, :first])
                if (b, a) == (0, 0):
                    nc.scalar.activation(out=dst[:, 0], in_=src[:, 0], func=COPY)
                    first = 1
                nc.scalar.copy(out=dst[:, first:], in_=src[:, first:])
            return rounded[:].rearrange("p t m j -> p (t m j)")

        def quantize(words, scales, values):
            nc.vector.quantize_mx(out=words.bitcast(FP8X4), scales=scales, in_=values)

        def quantize_w1(b, a, rounded, edges):
            for lo, hi in zip(edges, edges[1:]):
                quantize(w1_w[b][a][:, lo:hi], w1_s[b][a][:, lo:hi], rounded[:, PACK * lo : PACK * hi])

        def first_stage(b, t, half):
            rows = slice(t * P, (t + 1) * P)
            cols = slice(half * BANK, (half + 1) * BANK)
            acc = bank(2 * t + half, [P, BANK])
            for a in range(PASSES):
                nc.tensor.matmul_mx(
                    out=acc[:],
                    lhsT=w1_w[b][a][:, rows].bitcast(FP8X4),
                    lhsT_scale=w1_s[b][a][:, rows],
                    rhs=v_w[a][:, cols].bitcast(FP8X4),
                    rhs_scale=v_s[4 * a : P, cols],
                    start=(a == 0),
                    stop=(a == PASSES - 1),
                )
            g = gain_t[:, b, t : t + 1]
            if (b, t, half) == (0, 0, 1):
                nc.vector.tensor_scalar_mul(h[b][t][:, cols], acc[:], g)
            else:
                nc.scalar.activation(out=h[b][t][:, cols], in_=acc[:], func=COPY, scale=g)

        quantize_w1(0, 0, round_w1(0, 0, 0), (0, PASS))
        quantize_w1(0, 1, round_w1(0, 1, VECTOR_SHARE), (0, P, PASS))
        for t in range(PACK):
            for half in range(2):
                first_stage(0, t, half)
        for a in range(PASSES):
            quantize_w1(1, a, round_w1(1, a, 0), (0, PASS))
        for t in range(PACK):
            for half in range(2):
                first_stage(1, t, half)

        wa_raw = {}
        for b in range(PASSES):
            wa_raw[b] = slot_tile("words%d" % b, [P, PACK, N], F32)
            nc.sync.dma_start(out=wa_raw[b][:], in_=pass_rows(wa, b))
        nc.sync.dma_start(out=w4_w[:].bitcast(I32), in_=w4_words.rearrange("a p n -> p a n").bitcast(I32))
        nc.sync.dma_start(out=read_t[1][:], in_=pass_rows(reading, 1))
        for q in range(4):
            nc.sync.dma_start(
                out=w4_s[32 * q : 32 * q + 4, :, :].bitcast(I32),
                in_=w4_scales[:, 4 * q : 4 * q + 4, :].rearrange("a r n -> r a n").bitcast(I32),
            )

        def quantize_wa(b, u):
            rounded = slot_tile("fg"[u], [P, WA_COLS, PACK], BF16)
            cols = slice(u * WA_COLS, (u + 1) * WA_COLS)
            nc.scalar.activation(
                out=rounded[:].rearrange("p (c i) j -> p c j i", i=4),
                in_=wa_raw[b][:, :, cols].rearrange("p j (c i) -> p c j i", i=4),
                func=COPY,
            )
            quantize(wa_w[b][:, cols], wa_s[b][:, cols], rounded[:].rearrange("p c j -> p (c j)"))

        planes = {}
        held_back = {
            "c": [("lawn", 0, 0, 2)],
            "d": [("lawn", 0, 0, 3), ("edge", 0, 0, 2), ("edge", 0, 0, 3)],
            "lawn": [("lawn", 1, 0, t) for t in range(PACK)],
            "b": [("edge", 1, 0, t) for t in range(2)],
            "e": [("edge", 1, 0, t) for t in range(2, PACK)],
            "f": [("edge", 1, M_HALF, t) for t in range(PACK)],
        }
        places = {}
        groups = {}

        def pick(kind, b, lo, hi, t):
            for slot, group in held_back.items():
                if group[0] == (kind, b, lo, t):
                    shared = slot_tile(slot, [P, len(group), hi - lo], F32)
                    groups[slot] = shared
                    for i, member in enumerate(group):
                        places[member] = shared[:, i, :]
            if (kind, b, lo, t) in places:
                picked = places[kind, b, lo, t]
            else:
                picked = ring.tile([P, hi - lo], F32, name="picked", tag="picked", bufs=3)[:]
            pos_t = pos1_t if kind == "edge" else pos2_t
            nc.vector.tensor_copy(picked, h[b][t][:].indirect(pos_t[:, lo // 16 : hi // 16]))
            return picked

        def combine(kind, b, lo, hi, t, picked):
            if t == 0:
                planes[kind, b, lo] = ring.tile([P, PACK, hi - lo], BF16, name="planes", tag="planes_" + kind)
            dst = planes[kind, b, lo][:, t, :]
            if kind == "edge":
                nc.vector.scalar_tensor_tensor(
                    dst, picked, rim_t[:, b, t : t + 1], read_t[b][:, t, lo:hi], ALU.add, ALU.mult
                )
            else:
                nc.vector.tensor_scalar_max(dst, picked, floor_t[:, b, t : t + 1])

        def weave_and_quantize(kind, b, lo, hi, slot, copy=nc.scalar.copy):
            woven = slot_tile(slot, [P, hi - lo, PACK], BF16)
            copy(
                out=woven[:].rearrange("p (c i) t -> p c t i", i=4),
                in_=planes[kind, b, lo][:].rearrange("p t (c i) -> p c t i", i=4),
            )
            words, scales = (xa_w, xa_s) if kind == "edge" else (xb_w, xb_s)
            quantize(words[b][:, lo:hi], scales[b][:, lo:hi], woven[:].rearrange("p m t -> p (m t)"))

        def lawn_product():
            for n in range(N_TILES):
                yb = bank(n, [P, M])
                for b in range(PASSES):
                    nc.tensor.matmul_mx(
                        out=yb[:],
                        lhsT=w4_w[:, b, 2 * n * P : 2 * (n + 1) * P].bitcast(FP4X4),
                        lhsT_scale=w4_s[:, b, n * P : (n + 1) * P],
                        rhs=xb_w[b][:].bitcast(FP8X4),
                        rhs_scale=xb_s[b][:],
                        start=(b == 0),
                        stop=(b == PASSES - 1),
                    )
                nc.scalar.activation(out=res[:, n, :], in_=yb[:], func=COPY, bias=1.0)

        ya = {}

        def edge_pass(b, half):
            cols = slice(half * M_HALF, (half + 1) * M_HALF)
            for pair in range(N_TILES // 2):
                if b == 0:
                    ya[half, pair] = bank(3 * half + pair, [P, 2, M_HALF])
                for i in range(2):
                    rows = slice((2 * pair + i) * P, (2 * pair + i + 1) * P)
                    nc.tensor.matmul_mx(
                        out=ya[half, pair][:, i, :],
                        lhsT=wa_w[b][:, rows].bitcast(FP8X4),
                        lhsT_scale=wa_s[b][:, rows],
                        rhs=xa_w[b][:, cols].bitcast(FP8X4),
                        rhs_scale=xa_s[b][:, cols],
                        start=(b == 0 and i == 0),
                        stop=(b == PASSES - 1 and i == 1),
                    )

        def finish(half, lo, hi):
            cols = slice(half * M_HALF, (half + 1) * M_HALF)
            part = res[:, lo:hi, cols]
            nc.vector.tensor_tensor(part, ya[half, lo // 2][:, lo % 2 : lo % 2 + hi - lo, :], part, ALU.mult)
            nc.sync.dma_start(out=out[lo * P : hi * P, cols].rearrange("(i p) m -> p i m", p=P), in_=part)

        def after_first_group():
            weave_and_quantize("lawn", 0, 0, M, "a")
            weave_and_quantize("edge", 0, 0, M, "b")

        def after_lawn():
            weave_and_quantize("lawn", 1, 0, M, "e")
            for u in range(2):
                quantize_wa(1, u)
            lawn_product()
            for half in range(2):
                edge_pass(0, half)

        def after_edge(half):
            if half == 0:
                weave_and_quantize("edge", 1, 0, M_HALF, "h")
            else:
                weave_and_quantize("edge", 1, M_HALF, M, "h", nc.vector.tensor_copy)
            edge_pass(1, half)

        for u in range(2):
            quantize_wa(0, u)
        steps = [(kind, 0, 0, M, t) for t in range(2) for kind in ("lawn", "edge")]
        steps = steps + [(kind, 0, 0, M, t) for kind in ("lawn", "edge") for t in range(2, PACK)]
        steps = steps + [("lawn", 1, 0, M, t) for t in range(PACK)]
        steps = steps + [("edge", 1, half * M_HALF, (half + 1) * M_HALF, t) for half in range(2) for t in range(PACK)]
        then = {
            ("edge", 0, 0): after_first_group,
            ("lawn", 1, 0): after_lawn,
            ("edge", 1, 0): lambda: after_edge(0),
            ("edge", 1, M_HALF): lambda: after_edge(1),
        }
        picked = pick(*steps[0])
        for step, following in zip(steps, steps[1:] + [None]):
            ahead = pick(*following) if following else None
            combine(*step, picked)
            if step[4] == PACK - 1 and step[:3] in then:
                then[step[:3]]()
            picked = ahead
        for half, edges in enumerate(((0, 2, 4, 6), (0, 2, 4, 6))):
            for lo, hi in zip(edges, edges[1:]):
                finish(half, lo, hi)
